import numpy as np
import ml_dtypes


def mxq(x, axis, fmt="e4m3"):
    dtype, down = {"e4m3": (ml_dtypes.float8_e4m3fn, 7), "e5m2": (ml_dtypes.float8_e5m2, 14)}[fmt]
    v = np.moveaxis(np.asarray(x, np.float32).astype(ml_dtypes.bfloat16).astype(np.float64), axis, -1)
    blocks = v.reshape(v.shape[:-1] + (-1, 32))
    amax = np.abs(blocks).max(-1, keepdims=True)
    byte = np.maximum(np.where(amax > 0, np.frexp(amax)[1] - 1 + 127, 0) - down, 1)
    scale = np.exp2(byte - 127.0)
    codes = (blocks / scale).astype(np.float32).astype(dtype).astype(np.float64)
    return np.moveaxis((codes * scale).reshape(v.shape), -1, axis)


WIDE = False


def mx_kscale(k):
    if not WIDE:
        return np.ones(k)
    levels = np.array([10, -10, 5, -5, 0])
    if k % 512:
        return np.exp2(np.random.permutation(np.resize(levels, k // 32))).repeat(32)
    a = np.empty((k // 512, 16))
    for p in range(k // 512):
        a[p, :8] = np.random.permutation(np.resize(levels, 8))
        for g in range(8):
            far = levels[np.abs(levels - a[p, g]) >= 10]
            a[p, g + 8] = far[np.random.randint(len(far))]
    return np.exp2(a.ravel()).repeat(32)


BF16 = ml_dtypes.bfloat16


def bf(x):
    return np.asarray(x, np.float32).astype(BF16)


def f64(x):
    return np.asarray(x).astype(np.float64)

def planes(Y):
    n, m = Y.shape
    b = f64(bf(Y)).reshape(n // 32, 32, m)
    amax = np.abs(b).max(1)
    byte = np.clip(np.where(amax > 0, np.frexp(amax)[1] - 1 + 127 - 7, 1), 1, 254)
    codes = (b * np.exp2(127.0 - byte)[:, None, :]).reshape(n, m).astype(np.float32).astype(ml_dtypes.float8_e4m3fn).view(np.uint8)
    words = codes.reshape(n // 512, 128, 4, m).transpose(0, 1, 3, 2)
    return np.ascontiguousarray(words), np.ascontiguousarray(byte.astype(np.uint8).reshape(n // 512, 16, m))


P, T, S, NB = 2048, 512, 1536, 1024
RATE = 0.04
FIRST, LAST = 0.5, 30.0


def setup_inputs():
    rnd = np.random.randn
    s = mx_kscale(T)
    t = mx_kscale(P)
    size = np.exp(0.5 * rnd(P, 1))
    cashflows = size * rnd(P, T) / np.sqrt(T)
    years = np.linspace(FIRST, LAST, T)[:, None]
    rates = RATE * np.exp(0.5 * rnd(1, S) + 0.4 * rnd(T, S))
    discounts = np.exp(-rates * years)
    position_weights = np.exp(0.5 * rnd(P))
    bucket_map = np.exp(rnd(NB, P)) / P
    limit_weights = np.exp(0.8 * rnd(NB))
    return {
        "cashflows": bf(cashflows * s[None, :]),
        "discounts": bf(discounts / s[:, None]),
        "position_weights": bf(position_weights * t),
        "bucket_map": bf(bucket_map / t[None, :]),
        "limit_weights": bf(limit_weights),
    }


def reference(cashflows, discounts, position_weights, bucket_map, limit_weights):
    pv = mxq(f64(cashflows), 1, "e4m3") @ mxq(f64(discounts), 0, "e4m3")
    h = np.square(pv) * f64(position_weights)[:, None]
    v = mxq(f64(bucket_map), 1, "e4m3") @ mxq(h, 0, "e4m3")
    y = np.sqrt(v) * f64(limit_weights)[:, None]
    Y = y.reshape(NB, S)
    words, scales = planes(Y)
    return y, words, scales

@@ -1,0 +1,400 @@
+from contextlib import ExitStack
+
+import concourse.mybir as mybir
+from concourse.masks import make_identity
+
+POS, DATES, SCEN, BUCKETS = 2048, 512, 1536, 1024
+FLOPS = 2 * POS * DATES * SCEN + 2 * BUCKETS * POS * SCEN
+
+F32 = mybir.dt.float32
+BF16 = mybir.dt.bfloat16
+U32 = mybir.dt.uint32
+I32 = mybir.dt.int32
+U8 = mybir.dt.uint8
+FP8X4 = mybir.dt.float8_e4m3fn_x4
+ACT = mybir.ActivationFunctionType
+ALU = mybir.AluOpType
+
+P = 128
+PACK = 4
+W = 512
+POS_GROUPS = POS // W
+BUCKET_GROUPS = BUCKETS // W
+CHUNKS = SCEN // W
+RUN = 4
+HB = 8
+YB = 3
+HS = 3
+PIECES = [(0, 256), (256, 128), (384, 128)]
+
+
+def tile_bucketed_pv_limit_use_h3_kernel(
+    tc, cashflows, discounts, position_weights, bucket_map, limit_weights, out_0, out_1, out_2
+):
+    nc = tc.nc
+    with ExitStack() as ctx:
+        keep = ctx.enter_context(tc.tile_pool(name="keep", bufs=1))
+        flow = ctx.enter_context(tc.tile_pool(name="flow", bufs=3))
+        work = ctx.enter_context(tc.psum_pool(name="work", bufs=4))
+        sums = ctx.enter_context(tc.psum_pool(name="sums", bufs=4))
+        ctx.enter_context(tc.manual_schedule())
+
+        raw = {}
+        quantised = {}
+
+        def load(key, rows):
+            tile = keep.tile([P, PACK * W], BF16, name="raw_%s%d%d" % key, align_bytes=64)
+            nc.sync.dma_start(out=tile[:].rearrange("p (t n) -> p t n", t=PACK), in_=rows.rearrange("(p t) n -> p t n", t=PACK))
+            raw[key] = tile
+
+        def load_c_half(c, half):
+            key = ("c", c, 0)
+            if half == 0:
+                raw[key] = keep.tile([P, PACK * W], BF16, name="raw_%s%d%d" % key, align_bytes=64)
+            rows = cashflows[cols(c), :].rearrange("(p t) n -> p (t n)", t=PACK)
+            part = slice(2 * W * half, 2 * W * (half + 1))
+            nc.sync.dma_start(out=raw[key][:, part], in_=rows[:, part])
+
+        def cols(i):
+            return slice(W * i, W * (i + 1))
+
+        def load_c(c):
+            load(("c", c, 0), cashflows[cols(c), :])
+
+        def load_d(j):
+            load(("d", j, 0), discounts[:, cols(j)])
+
+        def load_b(g, c):
+            load(("b", g, c), bucket_map[cols(g), cols(c)])
+
+        w_raw = keep.tile([P, POS_GROUPS, PACK], BF16, name="w_raw")
+        nc.scalar.dma_start(out=w_raw[:], in_=position_weights.rearrange("(c p t) -> p c t", p=P, t=PACK))
+        lw_raw = keep.tile([P, BUCKET_GROUPS, PACK], BF16, name="lw_raw")
+        nc.scalar.dma_start(out=lw_raw[:], in_=limit_weights.rearrange("(g p t) -> p g t", p=P, t=PACK))
+        load_d(0)
+        load_c_half(0, 0)
+        load_c_half(0, 1)
+        load_c_half(1, 0)
+        load_c_half(1, 1)
+        load_b(0, 0)
+        load_c(2)
+        load_c(3)
+        load_d(1)
+        load_b(0, 1)
+        load_b(0, 2)
+        load_b(0, 3)
+        load_b(1, 0)
+        load_d(2)
+        load_b(1, 1)
+        load_b(1, 2)
+        load_b(1, 3)
+
+        ident = keep.tile([P, P], F32, name="ident")
+        make_identity(nc, ident[:])
+
+        warm_in = keep.tile([P, 1], F32, name="warm_in")
+        warm_out = keep.tile([P, 1], F32, name="warm_out")
+        nc.vector.memset(warm_in[:], 1.0)
+        nc.scalar.activation(out=warm_out[:], in_=warm_in[:], func=ACT.Sqrt)
+
+        n_w = POS_GROUPS * PACK
+        root0 = keep.tile([P, n_w], F32, name="root0")
+        inv = keep.tile([P, n_w], F32, name="inv")
+        half_q = keep.tile([P, n_w], F32, name="half_q")
+        root_w = keep.tile([P, n_w], F32, name="root_w")
+        lw_sq = keep.tile([P, BUCKET_GROUPS * PACK], F32, name="lw_sq")
+        w_flat = w_raw[:].rearrange("p c t -> p (c t)")
+        lw_flat = lw_raw[:].rearrange("p g t -> p (g t)")
+
+        def weights_1():
+            nc.scalar.activation(out=root0[:], in_=w_flat, func=ACT.Sqrt)
+            nc.vector.reciprocal(out=inv[:], in_=root0[:])
+            nc.vector.tensor_tensor(out=lw_sq[:], in0=lw_flat, in1=lw_flat, op=ALU.mult)
+            nc.vector.scalar_tensor_tensor(out=half_q[:], in0=w_flat, scalar=0.5, in1=inv[:], op0=ALU.mult, op1=ALU.mult)
+            nc.vector.scalar_tensor_tensor(out=root_w[:], in0=root0[:], scalar=0.5, in1=half_q[:], op0=ALU.mult, op1=ALU.add)
+
+        y_scales = keep.tile([P, SCEN], U8, name="y_scales", align_bytes=64)
+
+        def interleave(dst, src):
+            nc.vector.tensor_copy(
+                out=dst.rearrange("p (c i) t -> p c t i", i=RUN),
+                in_=src.rearrange("p t (c i) -> p c t i", i=RUN),
+            )
+
+        def quantise(key, grouped, bufs):
+            tag = key[0]
+            codes = flow.tile([P, W], U32, name="codes_%s%d%d" % key, tag="codes_" + tag, bufs=bufs, align_bytes=64)
+            scales = flow.tile([P, W], U8, name="scales_%s%d%d" % key, tag="scales_" + tag, bufs=bufs, align_bytes=64)
+            nc.vector.quantize_mx(out=codes[:].bitcast(FP8X4), scales=scales[:], in_=grouped)
+            quantised[key] = (codes, scales)
+
+        staged = {}
+        banks = {}
+        source = {key: tile[:].rearrange("p (t n) -> p t n", t=PACK) for key, tile in raw.items()}
+        KEEP = {"c": 4, "d": 3, "b": 8, "h": HB}
+
+        def turn(key, half):
+            words = raw[key][:].bitcast(F32)
+            bank = work.tile([P, 4, P], F32, name="bank", tag="bank")
+            for i in range(4):
+                t, u = 2 * half + i // 2, i % 2
+                nc.tensor.transpose(bank[:, i, :], words[:, 256 * t + u : 256 * (t + 1) : 2], ident[:])
+            banks[(key, half)] = bank
+
+        def unload(key, half, on_vector=False):
+            if key not in staged:
+                staged[key] = flow.tile([P, PACK * W], BF16, name="turned_%s%d%d" % key, tag="turned", bufs=4, align_bytes=64)
+            dst = staged[key][:, 1024 * half : 1024 * (half + 1)].bitcast(F32).rearrange("p (t m u) -> p t m u", t=2, u=2)
+            src = banks[(key, half)][:].rearrange("p (t u) m -> p t m u", u=2)
+            if on_vector:
+                nc.vector.tensor_copy(out=dst, in_=src)
+            else:
+                nc.scalar.copy(out=dst, in_=src)
+
+        def turn_s(key):
+            for half in range(2):
+                turn(key, half)
+                unload(key, half)
+
+        def pack(key):
+            grouped = flow.tile([P, W * PACK], BF16, name="packed_%s%d%d" % key, tag="packed", bufs=3, align_bytes=64)
+            interleave(grouped[:].rearrange("p (n t) -> p n t", t=PACK), source[key])
+            staged[key] = grouped
+
+        def quant_half(key, half):
+            if half == 0:
+                codes = flow.tile([P, W], U32, name="codes_%s%d%d" % key, tag="codes_c", bufs=4, align_bytes=64)
+                scales = flow.tile([P, W], U8, name="scales_%s%d%d" % key, tag="scales_c", bufs=4, align_bytes=64)
+                quantised[key] = (codes, scales)
+            codes, scales = quantised[key]
+            part = slice(256 * half, 256 * (half + 1))
+            nc.vector.quantize_mx(out=codes[:, part].bitcast(FP8X4), scales=scales[:, part], in_=staged[key][:, 1024 * half : 1024 * (half + 1)])
+
+        def pack_half(key, half):
+            if half == 0:
+                staged[key] = flow.tile([P, W * PACK], BF16, name="packed_%s%d%d" % key, tag="packed_d", bufs=1, align_bytes=64)
+            part = slice(256 * half, 256 * (half + 1))
+            interleave(staged[key][:].rearrange("p (n t) -> p n t", t=PACK)[:, part, :], source[key][:, :, part])
+
+        def quant(key):
+            if key[0] == "y":
+                planes(key[1], key[2], staged[key][:])
+            else:
+                quantise(key, staged[key][:], KEEP[key[0]])
+
+        def mx(out, lhs_key, t, rhs_key, start, stop, n=slice(0, W)):
+            lhs, lhs_scales = quantised[lhs_key]
+            rhs, rhs_scales = quantised[rhs_key]
+            m = slice(P * t, P * (t + 1))
+            nc.tensor.matmul_mx(
+                out=out, lhsT=lhs[:, m].bitcast(FP8X4), lhsT_scale=lhs_scales[:, m],
+                rhs=rhs[:, n].bitcast(FP8X4), rhs_scale=rhs_scales[:, n], start=start, stop=stop,
+            )
+
+        def squares(c, j, ts=range(PACK)):
+            if ("h", c, j) not in source:
+                source[("h", c, j)] = flow.tile([P, PACK, W], BF16, name="h_%d%d" % (c, j), tag="h", bufs=HS, align_bytes=64)[:]
+            h = source[("h", c, j)]
+            for t in ts:
+                bank = work.tile([P, W], F32, name="bank", tag="bank")
+                mx(bank[:], ("c", c, 0), t, ("d", j, 0), True, True)
+                i = PACK * c + t
+                nc.scalar.activation(out=h[:, t, :], in_=bank[:], func=ACT.Square, scale=root_w[:, i : i + 1])
+
+        acc = {}
+
+        def planes(g, j, grouped):
+            codes = flow.tile([P, W], U32, name="y_codes_%d%d" % (g, j), tag="y_codes", align_bytes=64)
+            nc.vector.quantize_mx(out=codes[:].bitcast(FP8X4), scales=y_scales[4 * g :, cols(j)], in_=grouped)
+            nc.sync.dma_start(
+                out=out_1[g, :, cols(j), :].rearrange("p n t -> p (n t)").bitcast(I32), in_=codes[:].bitcast(I32)
+            )
+
+        def root(g, j, t, bank):
+            if t == 0:
+                source[("y", g, j)] = flow.tile([P, PACK, W], F32, name="y_%d%d" % (g, j), tag="y", bufs=YB)[:]
+            y = source[("y", g, j)]
+            i = PACK * g + t
+            nc.scalar.activation(out=y[:, t, :], in_=bank[:], func=ACT.Sqrt, scale=lw_sq[:, i : i + 1])
+            rows = out_0[cols(g), cols(j)].rearrange("(p t) n -> p t n", t=PACK)
+            nc.sync.dma_start(out=rows[:, t, :], in_=y[:, t, :])
+
+        def one_pass(g, j, c, ts=range(PACK)):
+            for t in ts:
+                if c == 0:
+                    acc[(g, j, t)] = work.tile([P, W], F32, name="bank", tag="bank") if (g, j) == (0, 2) else sums.tile([P, W], F32, name="acc", tag="acc")
+                mx(acc[(g, j, t)][:], ("b", g, c), t, ("h", c, j), c == 0, c == POS_GROUPS - 1)
+
+        def roots(g, j, ts=range(PACK)):
+            for t in ts:
+                root(g, j, t, acc[(g, j, t)])
+
+        def passes(g, j, ts, cs):
+            for c in cs:
+                one_pass(g, j, c, ts)
+
+        def slots(g, j, ts):
+            for t in ts:
+                passes(g, j, (t,), range(POS_GROUPS))
+
+        def one_slot(g, j, t):
+            bank = sums.tile([P, W], F32, name="acc", tag="acc")
+            for c in range(POS_GROUPS):
+                mx(bank[:], ("b", g, c), t, ("h", c, j), c == 0, c == POS_GROUPS - 1)
+            root(g, j, t, bank)
+
+        def piece_sums(g, j, lo, width):
+            y = keep.tile([P, PACK, width], F32, name="y_piece_%d" % lo)
+            rows = out_0[cols(g), W * j + lo : W * j + lo + width].rearrange("(p t) n -> p t n", t=PACK)
+            for t in range(PACK):
+                bank = sums.tile([P, W], F32, name="acc", tag="acc")
+                for c in range(POS_GROUPS):
+                    mx(bank[:, :width], ("b", g, c), t, ("h", c, j), c == 0, c == POS_GROUPS - 1, slice(lo, lo + width))
+                i = PACK * g + t
+                nc.scalar.activation(out=y[:, t, :], in_=bank[:, :width], func=ACT.Sqrt, scale=lw_sq[:, i : i + 1])
+            nc.sync.dma_start(out=rows, in_=y[:])
+            return y
+
+        def piece_pack(y, lo, width):
+            grouped = keep.tile([P, width * PACK], BF16, name="packed_piece_%d" % lo, align_bytes=64)
+            interleave(grouped[:].rearrange("p (n t) -> p n t", t=PACK), y[:])
+            return grouped
+
+        def piece_planes(g, j, grouped, lo, width):
+            n = slice(W * j + lo, W * j + lo + width)
+            codes = keep.tile([P, width], U32, name="y_codes_piece_%d" % lo, align_bytes=64)
+            nc.vector.quantize_mx(out=codes[:].bitcast(FP8X4), scales=y_scales[4 * g :, n], in_=grouped[:])
+            nc.sync.dma_start(out=out_1[g, :, n, :].rearrange("p n t -> p (n t)").bitcast(I32), in_=codes[:].bitcast(I32))
+
+        def store_scales(n, queues):
+            for q in range(4):
+                queues[q % len(queues)].dma_start(
+                    out=out_2[:, 4 * q : 4 * q + 4, n].bitcast(I32),
+                    in_=y_scales[32 * q : 32 * q + 8, n].bitcast(I32),
+                )
+
+        def tv(key, on_vector):
+            for half in range(2):
+                turn(key, half)
+                unload(key, half, half in on_vector)
+
+        def C(c):
+            return ("c", c, 0)
+
+        def D(j):
+            return ("d", j, 0)
+
+        def B(g, c):
+            return ("b", g, c)
+
+        def H(c, j):
+            return ("h", c, j)
+
+        def Y(g, j):
+            return ("y", g, j)
+
+
+        A, Z = (0, 1), (2, 3)
+        weights_1()
+        pack(D(0))
+        tv(C(0), ())
+        quant(D(0))
+        quant_half(C(0), 0)
+        quant_half(C(0), 1)
+        tv(C(1), ())
+        squares(0, 0)
+        quant(C(1))
+        tv(B(0, 0), (0, 1))
+        pack(H(0, 0))
+        quant(B(0, 0))
+        squares(1, 0, A)
+        tv(C(2), ())
+        quant(H(0, 0))
+        squares(1, 0, Z)
+        quant(C(2))
+        tv(C(3), (0,))
+        pack(H(1, 0))
+        quant(C(3))
+        quant(H(1, 0))
+        pack_half(D(1), 0)
+        extra = {2: [lambda: pack_half(D(1), 1), lambda: quant(D(1))], 3: [lambda: pack_half(D(2), 0)], 4: [lambda: pack_half(D(2), 1)]}
+        for step, x, y in ((2, B(0, 1), B(0, 2)), (3, B(0, 3), B(1, 0)), (4, B(1, 1), B(1, 2))):
+            j, c = divmod(step, 4)
+            squares(c, j)
+            one_pass(0, 0, step - 2, A)
+            tv(x, (0,))
+            one_pass(0, 0, step - 2, Z)
+            pack(H(c, j))
+            quant(x)
+            tv(y, ())
+            quant(H(c, j))
+            for job in extra[step]:
+                job()
+            quant(y)
+        squares(1, 1)
+        one_pass(0, 0, 3, A)
+        tv(B(1, 3), (0, 1))
+        one_pass(0, 0, 3, Z)
+        quant(D(2))
+        quant(B(1, 3))
+        pack(H(1, 1))
+        roots(0, 0, A)
+        squares(2, 1)
+        slots(1, 0, A)
+        roots(0, 0, Z)
+        quant(H(1, 1))
+        pack(H(2, 1))
+        squares(3, 1)
+        slots(1, 0, Z)
+        roots(1, 0, A)
+        pack(Y(0, 0))
+        quant(H(2, 1))
+        pack(H(3, 1))
+        quant(Y(0, 0))
+        quant(H(3, 1))
+        squares(0, 2)
+        passes(0, 1, A, range(4))
+        roots(1, 0, Z)
+        pack(H(0, 2))
+        squares(1, 2)
+        slots(0, 1, Z)
+        roots(0, 1, A)
+        pack(Y(1, 0))
+        quant(H(0, 2))
+        pack(H(1, 2))
+        quant(Y(1, 0))
+        store_scales(cols(0), [nc.sync])
+        quant(H(1, 2))
+        squares(2, 2)
+        slots(1, 1, A)
+        roots(0, 1, Z)
+        pack(H(2, 2))
+        squares(3, 2)
+        slots(1, 1, Z)
+        roots(1, 1, A)
+        pack(Y(0, 1))
+        quant(H(2, 2))
+        pack(H(3, 2))
+        quant(Y(0, 1))
+        quant(H(3, 2))
+        passes(0, 2, A, range(3))
+        roots(1, 1, Z)
+        passes(0, 2, Z, range(3))
+        pack(Y(1, 1))
+        quant(Y(1, 1))
+        store_scales(cols(1), [nc.sync])
+        one_pass(0, 2, 3)
+        roots(0, 2)
+        (lo0, w0), (lo1, w1), (lo2, w2) = PIECES
+        y0 = piece_sums(1, 2, lo0, w0)
+        y1 = piece_sums(1, 2, lo1, w1)
+        pack(Y(0, 2))
+        p0 = piece_pack(y0, lo0, w0)
+        quant(Y(0, 2))
+        piece_planes(1, 2, p0, lo0, w0)
+        y2 = piece_sums(1, 2, lo2, w2)
+        p1 = piece_pack(y1, lo1, w1)
+        piece_planes(1, 2, p1, lo1, w1)
+        p2 = piece_pack(y2, lo2, w2)
+        piece_planes(1, 2, p2, lo2, w2)
+        store_scales(cols(2), [nc.scalar, nc.sync])

@@ -3,8 +3,8 @@ from contextlib import ExitStack
 import concourse.mybir as mybir
 from concourse.masks import make_identity
 
-POS, DATES, SCEN, BUCKETS = 2048, 512, 1536, 1024
-FLOPS = 2 * POS * DATES * SCEN + 2 * BUCKETS * POS * SCEN
+POSITIONS, DATES, SCENARIOS, BUCKETS = 2048, 512, 1536, 1024
+FLOPS = 2 * POSITIONS * DATES * SCENARIOS + 2 * BUCKETS * POSITIONS * SCENARIOS
 
 F32 = mybir.dt.float32
 BF16 = mybir.dt.bfloat16
@@ -16,16 +16,46 @@ ACT = mybir.ActivationFunctionType
 ALU = mybir.AluOpType
 
 P = 128
-PACK = 4
+SLOTS = 4
 W = 512
-POS_GROUPS = POS // W
+HALF = W // 2
+QUARTER = W // 4
+POS_GROUPS = POSITIONS // W
 BUCKET_GROUPS = BUCKETS // W
-CHUNKS = SCEN // W
+LAST_CHUNK = SCENARIOS // W - 1
 RUN = 4
-HB = 8
-YB = 3
-HS = 3
-PIECES = [(0, 256), (256, 128), (384, 128)]
+ALL_SLOTS = range(SLOTS)
+LOW, HIGH = (0, 1), (2, 3)
+ALL_GROUPS = range(POS_GROUPS)
+ALIVE = {"cash": POS_GROUPS, "disc": LAST_CHUNK + 1, "map": BUCKET_GROUPS * POS_GROUPS, "h": 2 * POS_GROUPS}
+
+
+def cash(c):
+    return ("cash", c)
+
+
+def disc(j):
+    return ("disc", j)
+
+
+def bmap(g, c):
+    return ("map", g, c)
+
+
+def h_of(c, j):
+    return ("h", c, j)
+
+
+def y_of(g, j, first=0, width=W):
+    return ("y", g, j, first, width)
+
+
+def label(prefix, key):
+    return "_".join([prefix] + [str(part) for part in key])
+
+
+def span(i, width=W):
+    return slice(width * i, width * (i + 1))
 
 
 def tile_bucketed_pv_limit_use_h3_kernel(
@@ -35,366 +65,346 @@ def tile_bucketed_pv_limit_use_h3_kernel(
     with ExitStack() as ctx:
         keep = ctx.enter_context(tc.tile_pool(name="keep", bufs=1))
         flow = ctx.enter_context(tc.tile_pool(name="flow", bufs=3))
-        work = ctx.enter_context(tc.psum_pool(name="work", bufs=4))
-        sums = ctx.enter_context(tc.psum_pool(name="sums", bufs=4))
+        work_pool = ctx.enter_context(tc.psum_pool(name="work", bufs=4))
+        sum_pool = ctx.enter_context(tc.psum_pool(name="sums", bufs=4))
         ctx.enter_context(tc.manual_schedule())
 
-        raw = {}
+        def work_bank():
+            return work_pool.tile([P, W], F32, name="work_bank")
+
+        def sum_bank():
+            return sum_pool.tile([P, W], F32, name="sum_bank")
+
+        rows_of = {}
+        sorted_words = {}
+        by_slot = {}
+        packed = {}
         quantised = {}
+        y_codes = {}
+        sums = {}
 
-        def load(key, rows):
-            tile = keep.tile([P, PACK * W], BF16, name="raw_%s%d%d" % key, align_bytes=64)
-            nc.sync.dma_start(out=tile[:].rearrange("p (t n) -> p t n", t=PACK), in_=rows.rearrange("(p t) n -> p t n", t=PACK))
-            raw[key] = tile
-
-        def load_c_half(c, half):
-            key = ("c", c, 0)
-            if half == 0:
-                raw[key] = keep.tile([P, PACK * W], BF16, name="raw_%s%d%d" % key, align_bytes=64)
-            rows = cashflows[cols(c), :].rearrange("(p t) n -> p (t n)", t=PACK)
-            part = slice(2 * W * half, 2 * W * (half + 1))
-            nc.sync.dma_start(out=raw[key][:, part], in_=rows[:, part])
-
-        def cols(i):
-            return slice(W * i, W * (i + 1))
-
-        def load_c(c):
-            load(("c", c, 0), cashflows[cols(c), :])
-
-        def load_d(j):
-            load(("d", j, 0), discounts[:, cols(j)])
-
-        def load_b(g, c):
-            load(("b", g, c), bucket_map[cols(g), cols(c)])
-
-        w_raw = keep.tile([P, POS_GROUPS, PACK], BF16, name="w_raw")
-        nc.scalar.dma_start(out=w_raw[:], in_=position_weights.rearrange("(c p t) -> p c t", p=P, t=PACK))
-        lw_raw = keep.tile([P, BUCKET_GROUPS, PACK], BF16, name="lw_raw")
-        nc.scalar.dma_start(out=lw_raw[:], in_=limit_weights.rearrange("(g p t) -> p g t", p=P, t=PACK))
-        load_d(0)
-        load_c_half(0, 0)
-        load_c_half(0, 1)
-        load_c_half(1, 0)
-        load_c_half(1, 1)
-        load_b(0, 0)
-        load_c(2)
-        load_c(3)
-        load_d(1)
-        load_b(0, 1)
-        load_b(0, 2)
-        load_b(0, 3)
-        load_b(1, 0)
-        load_d(2)
-        load_b(1, 1)
-        load_b(1, 2)
-        load_b(1, 3)
-
-        ident = keep.tile([P, P], F32, name="ident")
-        make_identity(nc, ident[:])
-
-        warm_in = keep.tile([P, 1], F32, name="warm_in")
-        warm_out = keep.tile([P, 1], F32, name="warm_out")
-        nc.vector.memset(warm_in[:], 1.0)
-        nc.scalar.activation(out=warm_out[:], in_=warm_in[:], func=ACT.Sqrt)
-
-        n_w = POS_GROUPS * PACK
-        root0 = keep.tile([P, n_w], F32, name="root0")
-        inv = keep.tile([P, n_w], F32, name="inv")
-        half_q = keep.tile([P, n_w], F32, name="half_q")
-        root_w = keep.tile([P, n_w], F32, name="root_w")
-        lw_sq = keep.tile([P, BUCKET_GROUPS * PACK], F32, name="lw_sq")
-        w_flat = w_raw[:].rearrange("p c t -> p (c t)")
-        lw_flat = lw_raw[:].rearrange("p g t -> p (g t)")
-
-        def weights_1():
-            nc.scalar.activation(out=root0[:], in_=w_flat, func=ACT.Sqrt)
-            nc.vector.reciprocal(out=inv[:], in_=root0[:])
-            nc.vector.tensor_tensor(out=lw_sq[:], in0=lw_flat, in1=lw_flat, op=ALU.mult)
-            nc.vector.scalar_tensor_tensor(out=half_q[:], in0=w_flat, scalar=0.5, in1=inv[:], op0=ALU.mult, op1=ALU.mult)
-            nc.vector.scalar_tensor_tensor(out=root_w[:], in0=root0[:], scalar=0.5, in1=half_q[:], op0=ALU.mult, op1=ALU.add)
-
-        y_scales = keep.tile([P, SCEN], U8, name="y_scales", align_bytes=64)
-
-        def interleave(dst, src):
-            nc.vector.tensor_copy(
-                out=dst.rearrange("p (c i) t -> p c t i", i=RUN),
-                in_=src.rearrange("p t (c i) -> p c t i", i=RUN),
+        def load_rows(key, rows):
+            rows_of[key] = keep.tile([P, SLOTS * W], BF16, name=label("rows", key), align_bytes=64)
+            nc.sync.dma_start(
+                out=rows_of[key][:].rearrange("p (t n) -> p t n", t=SLOTS), in_=rows.rearrange("(p t) n -> p t n", t=SLOTS)
             )
 
-        def quantise(key, grouped, bufs):
-            tag = key[0]
-            codes = flow.tile([P, W], U32, name="codes_%s%d%d" % key, tag="codes_" + tag, bufs=bufs, align_bytes=64)
-            scales = flow.tile([P, W], U8, name="scales_%s%d%d" % key, tag="scales_" + tag, bufs=bufs, align_bytes=64)
-            nc.vector.quantize_mx(out=codes[:].bitcast(FP8X4), scales=scales[:], in_=grouped)
-            quantised[key] = (codes, scales)
-
-        staged = {}
-        banks = {}
-        source = {key: tile[:].rearrange("p (t n) -> p t n", t=PACK) for key, tile in raw.items()}
-        KEEP = {"c": 4, "d": 3, "b": 8, "h": HB}
-
-        def turn(key, half):
-            words = raw[key][:].bitcast(F32)
-            bank = work.tile([P, 4, P], F32, name="bank", tag="bank")
-            for i in range(4):
-                t, u = 2 * half + i // 2, i % 2
-                nc.tensor.transpose(bank[:, i, :], words[:, 256 * t + u : 256 * (t + 1) : 2], ident[:])
-            banks[(key, half)] = bank
-
-        def unload(key, half, on_vector=False):
-            if key not in staged:
-                staged[key] = flow.tile([P, PACK * W], BF16, name="turned_%s%d%d" % key, tag="turned", bufs=4, align_bytes=64)
-            dst = staged[key][:, 1024 * half : 1024 * (half + 1)].bitcast(F32).rearrange("p (t m u) -> p t m u", t=2, u=2)
-            src = banks[(key, half)][:].rearrange("p (t u) m -> p t m u", u=2)
-            if on_vector:
-                nc.vector.tensor_copy(out=dst, in_=src)
-            else:
-                nc.scalar.copy(out=dst, in_=src)
-
-        def turn_s(key):
-            for half in range(2):
-                turn(key, half)
-                unload(key, half)
-
-        def pack(key):
-            grouped = flow.tile([P, W * PACK], BF16, name="packed_%s%d%d" % key, tag="packed", bufs=3, align_bytes=64)
-            interleave(grouped[:].rearrange("p (n t) -> p n t", t=PACK), source[key])
-            staged[key] = grouped
-
-        def quant_half(key, half):
+        def load_cash_half(c, half):
             if half == 0:
-                codes = flow.tile([P, W], U32, name="codes_%s%d%d" % key, tag="codes_c", bufs=4, align_bytes=64)
-                scales = flow.tile([P, W], U8, name="scales_%s%d%d" % key, tag="scales_c", bufs=4, align_bytes=64)
+                rows_of[cash(c)] = keep.tile([P, SLOTS * W], BF16, name=label("rows", cash(c)), align_bytes=64)
+            rows = cashflows[span(c), :].rearrange("(p t) n -> p (t n)", t=SLOTS)
+            nc.sync.dma_start(out=rows_of[cash(c)][:, span(half, 2 * W)], in_=rows[:, span(half, 2 * W)])
+
+        def load_disc(j, half=None):
+            cols = span(j) if half is None else span(2 * j + half, HALF)
+            width = cols.stop - cols.start
+            tile = keep.tile([P, SLOTS, width], BF16, name=label("rows", ("disc", cols.start)), align_bytes=64)
+            nc.sync.dma_start(out=tile[:], in_=discounts[:, cols].rearrange("(p t) n -> p t n", t=SLOTS))
+            by_slot[(disc(j), half)] = tile
+
+        def load_map(g, c):
+            load_rows(bmap(g, c), bucket_map[span(g), span(c)])
+
+        weight_rows = keep.tile([P, W], BF16, name="weight_rows", align_bytes=64)
+        nc.gpsimd.memset(weight_rows[:].bitcast(I32), 0)
+        n_rows = POS_GROUPS + BUCKET_GROUPS
+
+        load_cash_half(0, 0)
+        nc.sync.dma_start(out=weight_rows[:POS_GROUPS, :], in_=position_weights.rearrange("(c n) -> c n", n=W))
+        nc.sync.dma_start(out=weight_rows[POS_GROUPS:n_rows, :], in_=limit_weights.rearrange("(g n) -> g n", n=W))
+        load_disc(0, 0)
+        load_cash_half(0, 1)
+        load_disc(0, 1)
+        load_cash_half(1, 0)
+        load_cash_half(1, 1)
+        load_rows(cash(2), cashflows[span(2), :])
+        load_map(0, 0)
+        load_rows(cash(3), cashflows[span(3), :])
+        load_map(0, 1)
+        load_map(0, 2)
+        load_disc(1)
+        load_map(0, 3)
+        for c in ALL_GROUPS:
+            load_map(1, c)
+        load_disc(2)
+
+        identity = keep.tile([P, P], F32, name="identity")
+        make_identity(nc, identity[:])
+
+        one = keep.tile([P, 1], F32, name="one")
+        root_of_one = keep.tile([P, 1], F32, name="root_of_one")
+        nc.vector.memset(one[:], 1.0)
+        nc.scalar.activation(out=root_of_one[:], in_=one[:], func=ACT.Sqrt)
+
+        n_w = POS_GROUPS * SLOTS
+        weights = keep.tile([P, n_rows * SLOTS], BF16, name="weights", align_bytes=64)
+        w, limit = weights[:, :n_w], weights[:, n_w:]
+        guess = keep.tile([P, n_w], F32, name="guess")
+        inverse = keep.tile([P, n_w], F32, name="inverse")
+        half_quotient = keep.tile([P, n_w], F32, name="half_quotient")
+        root_w = keep.tile([P, n_w], F32, name="root_w")
+        limit_squared = keep.tile([P, BUCKET_GROUPS * SLOTS], F32, name="limit_squared")
+
+        def turn_weights():
+            bank = work_bank()[:].rearrange("p (u r) -> p u r", r=P)
+            words = weight_rows[:].bitcast(F32)
+            for u in range(2):
+                nc.tensor.transpose(bank[:, u, :], words[:, u::2], identity[:])
+            nc.vector.tensor_copy(
+                out=weights[:].bitcast(F32).rearrange("p (r u) -> p r u", u=2),
+                in_=bank[:, :2, :n_rows].rearrange("p u r -> p r u"),
+            )
+
+        y_scales = keep.tile([P, SCENARIOS], U8, name="y_scales", align_bytes=64)
+
+        def sort_words(key):
+            tile = flow.tile([P, SLOTS, 2, P], F32, name=label("sorted", key), tag="sorted", align_bytes=64)
+            nc.vector.tensor_copy(out=tile[:], in_=rows_of[key][:].bitcast(F32).rearrange("p (t m u) -> p t u m", t=SLOTS, u=2))
+            sorted_words[key] = tile
+
+        def turn(key, half, bank, on_vector):
+            bank = bank[:].rearrange("p (t u m) -> p t u m", t=2, u=2)
+            words = rows_of[key][:].bitcast(F32).rearrange("p (t m u) -> p t u m", t=SLOTS, u=2)
+            if key in sorted_words:
+                words = sorted_words[key][:]
+            for t in range(2):
+                for u in range(2):
+                    nc.tensor.transpose(bank[:, t, u, :], words[:, 2 * half + t, u, :], identity[:])
+            if half == 0:
+                packed[key] = flow.tile([P, SLOTS * W], BF16, name=label("turned", key), tag="turned", align_bytes=64)
+            out = packed[key][:, span(half, 2 * W)].bitcast(F32).rearrange("p (t m u) -> p t m u", t=2, u=2)
+            if on_vector:
+                nc.vector.tensor_copy(out=out, in_=bank.rearrange("p t u m -> p t m u"))
+            else:
+                nc.scalar.copy(out=out, in_=bank.rearrange("p t u m -> p t m u"))
+
+        def turn_both(key, new_bank, halves_on_vector=()):
+            for half in range(2):
+                turn(key, half, new_bank(), half in halves_on_vector)
+
+        def pack(key, half=None):
+            source = by_slot[(key, half)]
+            width = source.shape[2]
+            if half != 1:
+                whole = width if half is None else 2 * width
+                packed[key] = flow.tile([P, whole * SLOTS], BF16, name=label("packed", key), tag="packed", align_bytes=64)
+            out = packed[key][:, span(half or 0, width * SLOTS)]
+            nc.vector.tensor_copy(
+                out=out.rearrange("p (c i t) -> p c t i", i=RUN, t=SLOTS),
+                in_=source[:].rearrange("p t (c i) -> p c t i", i=RUN),
+            )
+
+        def quantise(key, half=None):
+            if half != 1:
+                kind = key[0]
+                codes = flow.tile([P, W], U32, name=label("codes", key), tag="codes_" + kind, bufs=ALIVE[kind], align_bytes=64)
+                scales = flow.tile([P, W], U8, name=label("scales", key), tag="scales_" + kind, bufs=ALIVE[kind], align_bytes=64)
                 quantised[key] = (codes, scales)
             codes, scales = quantised[key]
-            part = slice(256 * half, 256 * (half + 1))
-            nc.vector.quantize_mx(out=codes[:, part].bitcast(FP8X4), scales=scales[:, part], in_=staged[key][:, 1024 * half : 1024 * (half + 1)])
+            cols, width = (span(0), W) if half is None else (span(half, HALF), HALF)
+            nc.vector.quantize_mx(
+                out=codes[:, cols].bitcast(FP8X4), scales=scales[:, cols], in_=packed[key][:, span(half or 0, width * SLOTS)]
+            )
 
-        def pack_half(key, half):
-            if half == 0:
-                staged[key] = flow.tile([P, W * PACK], BF16, name="packed_%s%d%d" % key, tag="packed_d", bufs=1, align_bytes=64)
-            part = slice(256 * half, 256 * (half + 1))
-            interleave(staged[key][:].rearrange("p (n t) -> p n t", t=PACK)[:, part, :], source[key][:, :, part])
-
-        def quant(key):
-            if key[0] == "y":
-                planes(key[1], key[2], staged[key][:])
-            else:
-                quantise(key, staged[key][:], KEEP[key[0]])
-
-        def mx(out, lhs_key, t, rhs_key, start, stop, n=slice(0, W)):
-            lhs, lhs_scales = quantised[lhs_key]
-            rhs, rhs_scales = quantised[rhs_key]
-            m = slice(P * t, P * (t + 1))
+        def matmul(out, stationary, slot, moving, cols, start, stop):
+            lhs, lhs_scales = quantised[stationary]
+            rhs, rhs_scales = quantised[moving]
             nc.tensor.matmul_mx(
-                out=out, lhsT=lhs[:, m].bitcast(FP8X4), lhsT_scale=lhs_scales[:, m],
-                rhs=rhs[:, n].bitcast(FP8X4), rhs_scale=rhs_scales[:, n], start=start, stop=stop,
+                out=out,
+                lhsT=lhs[:, span(slot, P)].bitcast(FP8X4),
+                lhsT_scale=lhs_scales[:, span(slot, P)],
+                rhs=rhs[:, cols].bitcast(FP8X4),
+                rhs_scale=rhs_scales[:, cols],
+                start=start,
+                stop=stop,
             )
 
-        def squares(c, j, ts=range(PACK)):
-            if ("h", c, j) not in source:
-                source[("h", c, j)] = flow.tile([P, PACK, W], BF16, name="h_%d%d" % (c, j), tag="h", bufs=HS, align_bytes=64)[:]
-            h = source[("h", c, j)]
-            for t in ts:
-                bank = work.tile([P, W], F32, name="bank", tag="bank")
-                mx(bank[:], ("c", c, 0), t, ("d", j, 0), True, True)
-                i = PACK * c + t
-                nc.scalar.activation(out=h[:, t, :], in_=bank[:], func=ACT.Square, scale=root_w[:, i : i + 1])
+        def squares(c, j, half=None):
+            cols, width = (span(0), W) if half is None else (span(half, HALF), HALF)
+            h = flow.tile([P, SLOTS, width], BF16, name=label("h", (c, j, width)), tag="h", align_bytes=64)
+            for t in ALL_SLOTS:
+                bank = work_bank()
+                matmul(bank[:, :width], cash(c), t, disc(j), cols, True, True)
+                i = SLOTS * c + t
+                nc.scalar.activation(out=h[:, t, :], in_=bank[:, :width], func=ACT.Square, scale=root_w[:, i : i + 1])
+            by_slot[(h_of(c, j), half)] = h
 
-        acc = {}
+        def passes(y, slots, groups, new_bank=sum_bank):
+            kind, g, j, first, width = y
+            for c in groups:
+                for t in slots:
+                    if c == 0:
+                        sums[(y, t)] = new_bank()
+                    cols = slice(first, first + width)
+                    matmul(sums[(y, t)][:, :width], bmap(g, c), t, h_of(c, j), cols, c == 0, c == POS_GROUPS - 1)
 
-        def planes(g, j, grouped):
-            codes = flow.tile([P, W], U32, name="y_codes_%d%d" % (g, j), tag="y_codes", align_bytes=64)
-            nc.vector.quantize_mx(out=codes[:].bitcast(FP8X4), scales=y_scales[4 * g :, cols(j)], in_=grouped)
-            nc.sync.dma_start(
-                out=out_1[g, :, cols(j), :].rearrange("p n t -> p (n t)").bitcast(I32), in_=codes[:].bitcast(I32)
-            )
+        def slot_sums(y, slots, new_bank=sum_bank):
+            for t in slots:
+                passes(y, (t,), ALL_GROUPS, new_bank)
 
-        def root(g, j, t, bank):
-            if t == 0:
-                source[("y", g, j)] = flow.tile([P, PACK, W], F32, name="y_%d%d" % (g, j), tag="y", bufs=YB)[:]
-            y = source[("y", g, j)]
-            i = PACK * g + t
-            nc.scalar.activation(out=y[:, t, :], in_=bank[:], func=ACT.Sqrt, scale=lw_sq[:, i : i + 1])
-            rows = out_0[cols(g), cols(j)].rearrange("(p t) n -> p t n", t=PACK)
-            nc.sync.dma_start(out=rows[:, t, :], in_=y[:, t, :])
+        def roots(y, slots):
+            kind, g, j, first, width = y
+            if 0 in slots:
+                tag, bufs = ("y", 2) if width == W else ("y_piece", 5)
+                by_slot[(y, None)] = flow.tile([P, SLOTS, width], F32, name=label("values", y), tag=tag, bufs=bufs)
+            values = by_slot[(y, None)]
+            rows = out_0[span(g), W * j + first : W * j + first + width].rearrange("(p t) n -> p t n", t=SLOTS)
+            together = W // width
+            for t in slots:
+                i = SLOTS * g + t
+                nc.scalar.activation(
+                    out=values[:, t, :], in_=sums[(y, t)][:, :width], func=ACT.Sqrt, scale=limit_squared[:, i : i + 1]
+                )
+                if (t + 1) % together == 0:
+                    done = slice(t + 1 - together, t + 1)
+                    nc.sync.dma_start(out=rows[:, done, :], in_=values[:, done, :])
 
-        def one_pass(g, j, c, ts=range(PACK)):
-            for t in ts:
-                if c == 0:
-                    acc[(g, j, t)] = work.tile([P, W], F32, name="bank", tag="bank") if (g, j) == (0, 2) else sums.tile([P, W], F32, name="acc", tag="acc")
-                mx(acc[(g, j, t)][:], ("b", g, c), t, ("h", c, j), c == 0, c == POS_GROUPS - 1)
+        def sums_and_roots(y, new_bank):
+            for t in ALL_SLOTS:
+                slot_sums(y, (t,), new_bank)
+                roots(y, (t,))
 
-        def roots(g, j, ts=range(PACK)):
-            for t in ts:
-                root(g, j, t, acc[(g, j, t)])
+        def quantise_y(y):
+            kind, g, j, first, width = y
+            cols = slice(W * j + first, W * j + first + width)
+            codes = flow.tile([P, width], U32, name=label("codes", y), tag="codes_y", bufs=4, align_bytes=64)
+            nc.vector.quantize_mx(out=codes[:].bitcast(FP8X4), scales=y_scales[4 * g :, cols], in_=packed[y][:])
+            y_codes[y] = codes
 
-        def passes(g, j, ts, cs):
-            for c in cs:
-                one_pass(g, j, c, ts)
+        def store_codes(y):
+            kind, g, j, first, width = y
+            cols = slice(W * j + first, W * j + first + width)
+            nc.sync.dma_start(out=out_1[g, :, cols, :].rearrange("p n t -> p (n t)").bitcast(I32), in_=y_codes[y][:].bitcast(I32))
 
-        def slots(g, j, ts):
-            for t in ts:
-                passes(g, j, (t,), range(POS_GROUPS))
-
-        def one_slot(g, j, t):
-            bank = sums.tile([P, W], F32, name="acc", tag="acc")
-            for c in range(POS_GROUPS):
-                mx(bank[:], ("b", g, c), t, ("h", c, j), c == 0, c == POS_GROUPS - 1)
-            root(g, j, t, bank)
-
-        def piece_sums(g, j, lo, width):
-            y = keep.tile([P, PACK, width], F32, name="y_piece_%d" % lo)
-            rows = out_0[cols(g), W * j + lo : W * j + lo + width].rearrange("(p t) n -> p t n", t=PACK)
-            for t in range(PACK):
-                bank = sums.tile([P, W], F32, name="acc", tag="acc")
-                for c in range(POS_GROUPS):
-                    mx(bank[:, :width], ("b", g, c), t, ("h", c, j), c == 0, c == POS_GROUPS - 1, slice(lo, lo + width))
-                i = PACK * g + t
-                nc.scalar.activation(out=y[:, t, :], in_=bank[:, :width], func=ACT.Sqrt, scale=lw_sq[:, i : i + 1])
-            nc.sync.dma_start(out=rows, in_=y[:])
-            return y
-
-        def piece_pack(y, lo, width):
-            grouped = keep.tile([P, width * PACK], BF16, name="packed_piece_%d" % lo, align_bytes=64)
-            interleave(grouped[:].rearrange("p (n t) -> p n t", t=PACK), y[:])
-            return grouped
-
-        def piece_planes(g, j, grouped, lo, width):
-            n = slice(W * j + lo, W * j + lo + width)
-            codes = keep.tile([P, width], U32, name="y_codes_piece_%d" % lo, align_bytes=64)
-            nc.vector.quantize_mx(out=codes[:].bitcast(FP8X4), scales=y_scales[4 * g :, n], in_=grouped[:])
-            nc.sync.dma_start(out=out_1[g, :, n, :].rearrange("p n t -> p (n t)").bitcast(I32), in_=codes[:].bitcast(I32))
-
-        def store_scales(n, queues):
+        def store_scales(cols, queues):
             for q in range(4):
                 queues[q % len(queues)].dma_start(
-                    out=out_2[:, 4 * q : 4 * q + 4, n].bitcast(I32),
-                    in_=y_scales[32 * q : 32 * q + 8, n].bitcast(I32),
+                    out=out_2[:, 4 * q : 4 * q + 4, cols].bitcast(I32),
+                    in_=y_scales[32 * q : 32 * q + 8, cols].bitcast(I32),
                 )
 
-        def tv(key, on_vector):
-            for half in range(2):
-                turn(key, half)
-                unload(key, half, half in on_vector)
 
-        def C(c):
-            return ("c", c, 0)
+        pack(disc(0), 0)
+        turn(cash(0), 0, sum_bank(), False)
+        turn_weights()
+        nc.scalar.activation(out=guess[:], in_=w, func=ACT.Sqrt)
+        turn(cash(0), 1, sum_bank(), False)
+        quantise(cash(0), 0)
+        pack(disc(0), 1)
+        nc.vector.reciprocal(out=inverse[:], in_=guess[:])
+        quantise(disc(0))
+        nc.vector.scalar_tensor_tensor(out=half_quotient[:], in0=w, scalar=0.5, in1=inverse[:], op0=ALU.mult, op1=ALU.mult)
+        quantise(cash(0), 1)
+        nc.vector.scalar_tensor_tensor(out=root_w[:], in0=guess[:], scalar=0.5, in1=half_quotient[:], op0=ALU.mult, op1=ALU.add)
+        nc.vector.tensor_tensor(out=limit_squared[:], in0=limit, in1=limit, op=ALU.mult)
+        turn_both(cash(1), sum_bank)
 
-        def D(j):
-            return ("d", j, 0)
-
-        def B(g, c):
-            return ("b", g, c)
-
-        def H(c, j):
-            return ("h", c, j)
-
-        def Y(g, j):
-            return ("y", g, j)
-
-
-        A, Z = (0, 1), (2, 3)
-        weights_1()
-        pack(D(0))
-        tv(C(0), ())
-        quant(D(0))
-        quant_half(C(0), 0)
-        quant_half(C(0), 1)
-        tv(C(1), ())
+        sort_words(cash(2))
         squares(0, 0)
-        quant(C(1))
-        tv(B(0, 0), (0, 1))
-        pack(H(0, 0))
-        quant(B(0, 0))
-        squares(1, 0, A)
-        tv(C(2), ())
-        quant(H(0, 0))
-        squares(1, 0, Z)
-        quant(C(2))
-        tv(C(3), (0,))
-        pack(H(1, 0))
-        quant(C(3))
-        quant(H(1, 0))
-        pack_half(D(1), 0)
-        extra = {2: [lambda: pack_half(D(1), 1), lambda: quant(D(1))], 3: [lambda: pack_half(D(2), 0)], 4: [lambda: pack_half(D(2), 1)]}
-        for step, x, y in ((2, B(0, 1), B(0, 2)), (3, B(0, 3), B(1, 0)), (4, B(1, 1), B(1, 2))):
-            j, c = divmod(step, 4)
+        quantise(cash(1))
+        sort_words(bmap(0, 0))
+        sort_words(cash(3))
+        turn_both(cash(2), sum_bank, (0,))
+        turn_both(bmap(0, 0), sum_bank, (0,))
+        quantise(cash(2))
+        squares(1, 0)
+        pack(h_of(0, 0))
+        quantise(h_of(0, 0))
+        quantise(bmap(0, 0))
+        turn_both(cash(3), sum_bank, (0,))
+        pack(h_of(1, 0))
+        quantise(cash(3))
+        quantise(h_of(1, 0))
+
+        y00, y10, y01, y11 = y_of(0, 0), y_of(1, 0), y_of(0, 1), y_of(1, 1)
+        to_turn = [bmap(0, c) for c in range(1, POS_GROUPS)] + [bmap(1, c) for c in ALL_GROUPS]
+        to_sort = [bmap(1, c) for c in ALL_GROUPS]
+        for step, (c, j) in enumerate([(2, 0), (3, 0), (0, 1)]):
+            early, late = to_turn[2 * step], to_turn[2 * step + 1]
             squares(c, j)
-            one_pass(0, 0, step - 2, A)
-            tv(x, (0,))
-            one_pass(0, 0, step - 2, Z)
-            pack(H(c, j))
-            quant(x)
-            tv(y, ())
-            quant(H(c, j))
-            for job in extra[step]:
-                job()
-            quant(y)
+            passes(y00, LOW, (step,))
+            turn_both(early, work_bank)
+            passes(y00, HIGH, (step,))
+            pack(h_of(c, j))
+            if step > 0:
+                sort_words(to_sort[2 * step - 1])
+            quantise(early)
+            turn_both(late, work_bank)
+            if step == 0:
+                pack(disc(1))
+            quantise(h_of(c, j))
+            if step == 0:
+                quantise(disc(1))
+            if step < 2:
+                sort_words(to_sort[2 * step])
+            quantise(late)
+
         squares(1, 1)
-        one_pass(0, 0, 3, A)
-        tv(B(1, 3), (0, 1))
-        one_pass(0, 0, 3, Z)
-        quant(D(2))
-        quant(B(1, 3))
-        pack(H(1, 1))
-        roots(0, 0, A)
-        squares(2, 1)
-        slots(1, 0, A)
-        roots(0, 0, Z)
-        quant(H(1, 1))
-        pack(H(2, 1))
-        squares(3, 1)
-        slots(1, 0, Z)
-        roots(1, 0, A)
-        pack(Y(0, 0))
-        quant(H(2, 1))
-        pack(H(3, 1))
-        quant(Y(0, 0))
-        quant(H(3, 1))
-        squares(0, 2)
-        passes(0, 1, A, range(4))
-        roots(1, 0, Z)
-        pack(H(0, 2))
-        squares(1, 2)
-        slots(0, 1, Z)
-        roots(0, 1, A)
-        pack(Y(1, 0))
-        quant(H(0, 2))
-        pack(H(1, 2))
-        quant(Y(1, 0))
-        store_scales(cols(0), [nc.sync])
-        quant(H(1, 2))
-        squares(2, 2)
-        slots(1, 1, A)
-        roots(0, 1, Z)
-        pack(H(2, 2))
-        squares(3, 2)
-        slots(1, 1, Z)
-        roots(1, 1, A)
-        pack(Y(0, 1))
-        quant(H(2, 2))
-        pack(H(3, 2))
-        quant(Y(0, 1))
-        quant(H(3, 2))
-        passes(0, 2, A, range(3))
-        roots(1, 1, Z)
-        passes(0, 2, Z, range(3))
-        pack(Y(1, 1))
-        quant(Y(1, 1))
-        store_scales(cols(1), [nc.sync])
-        one_pass(0, 2, 3)
-        roots(0, 2)
-        (lo0, w0), (lo1, w1), (lo2, w2) = PIECES
-        y0 = piece_sums(1, 2, lo0, w0)
-        y1 = piece_sums(1, 2, lo1, w1)
-        pack(Y(0, 2))
-        p0 = piece_pack(y0, lo0, w0)
-        quant(Y(0, 2))
-        piece_planes(1, 2, p0, lo0, w0)
-        y2 = piece_sums(1, 2, lo2, w2)
-        p1 = piece_pack(y1, lo1, w1)
-        piece_planes(1, 2, p1, lo1, w1)
-        p2 = piece_pack(y2, lo2, w2)
-        piece_planes(1, 2, p2, lo2, w2)
-        store_scales(cols(2), [nc.scalar, nc.sync])
+        passes(y00, LOW, (3,))
+        turn_both(to_turn[-1], work_bank, (0, 1))
+        passes(y00, HIGH, (3,))
+        quantise(to_turn[-1])
+        roots(y00, LOW)
+        pack(disc(2))
+        pack(h_of(1, 1))
+        quantise(disc(2))
+        quantise(h_of(1, 1))
+
+        before = (y00, HIGH)
+        finished = waiting = None
+        for c, j, y, slots in [(2, 1, y10, LOW), (3, 1, y10, HIGH), (0, 2, y01, LOW), (1, 2, y01, HIGH), (2, 2, y11, LOW)]:
+            squares(c, j)
+            if (y, slots) == (y01, LOW):
+                passes(y, slots, ALL_GROUPS)
+            else:
+                slot_sums(y, slots)
+            roots(*before)
+            if waiting:
+                store_codes(waiting)
+            pack(h_of(c, j))
+            quantise(h_of(c, j))
+            if finished:
+                pack(finished)
+                quantise_y(finished)
+            waiting = finished
+            finished = before[0] if before[1] == HIGH else None
+            before = (y, slots)
+        store_scales(span(0), [nc.sync])
+
+        squares(3, 2, 0)
+        slot_sums(y11, (2,))
+        squares(3, 2, 1)
+        slot_sums(y11, (3,))
+        roots(y11, LOW)
+        pack(h_of(3, 2), 0)
+        pack(y01)
+        quantise(h_of(3, 2), 0)
+        pack(h_of(3, 2), 1)
+        quantise_y(y01)
+        quantise(h_of(3, 2), 1)
+
+        pieces = [
+            y_of(0, LAST_CHUNK, 0, HALF),
+            y_of(1, LAST_CHUNK, 0, HALF),
+            y_of(0, LAST_CHUNK, HALF, HALF),
+            y_of(1, LAST_CHUNK, HALF, QUARTER),
+            y_of(1, LAST_CHUNK, HALF + QUARTER, QUARTER),
+        ]
+        passes(pieces[0], ALL_SLOTS, ALL_GROUPS, work_bank)
+        roots(y11, HIGH)
+        store_codes(y01)
+        roots(pieces[0], ALL_SLOTS)
+        pack(y11)
+        pack(pieces[0])
+        quantise_y(y11)
+        quantise_y(pieces[0])
+        for k in range(1, len(pieces)):
+            new_bank = sum_bank if k % 2 else work_bank
+            sums_and_roots(pieces[k], new_bank)
+            if k == 1:
+                store_codes(y11)
+            store_codes(pieces[k - 1])
+            pack(pieces[k])
+            quantise_y(pieces[k])
+        store_codes(pieces[-1])
+        store_scales(slice(W, SCENARIOS), [nc.scalar, nc.sync])

@@ -27,6 +27,7 @@ RUN = 4
 ALL_SLOTS = range(SLOTS)
 LOW, HIGH = (0, 1), (2, 3)
 ALL_GROUPS = range(POS_GROUPS)
+SHARED_H = (0, LAST_CHUNK)
 ALIVE = {"cash": POS_GROUPS, "disc": LAST_CHUNK + 1, "map": BUCKET_GROUPS * POS_GROUPS, "h": 2 * POS_GROUPS}
 
 
@@ -81,6 +82,7 @@ def tile_bucketed_pv_limit_use_h3_kernel(
         packed = {}
         quantised = {}
         y_codes = {}
+        to_square = {}
         sums = {}
 
         def load_rows(key, rows):
@@ -130,11 +132,6 @@ def tile_bucketed_pv_limit_use_h3_kernel(
 
         identity = keep.tile([P, P], F32, name="identity")
         make_identity(nc, identity[:])
-
-        one = keep.tile([P, 1], F32, name="one")
-        root_of_one = keep.tile([P, 1], F32, name="root_of_one")
-        nc.vector.memset(one[:], 1.0)
-        nc.scalar.activation(out=root_of_one[:], in_=one[:], func=ACT.Sqrt)
 
         n_w = POS_GROUPS * SLOTS
         weights = keep.tile([P, n_rows * SLOTS], BF16, name="weights", align_bytes=64)
@@ -219,14 +216,21 @@ def tile_bucketed_pv_limit_use_h3_kernel(
                 stop=stop,
             )
 
-        def squares(c, j, half=None):
+        def squares(c, j, half=None, slots_on_scalar=ALL_SLOTS):
             cols, width = (span(0), W) if half is None else (span(half, HALF), HALF)
             h = flow.tile([P, SLOTS, width], BF16, name=label("h", (c, j, width)), tag="h", align_bytes=64)
             for t in ALL_SLOTS:
                 bank = work_bank()
                 matmul(bank[:, :width], cash(c), t, disc(j), cols, True, True)
                 i = SLOTS * c + t
-                nc.scalar.activation(out=h[:, t, :], in_=bank[:, :width], func=ACT.Square, scale=root_w[:, i : i + 1])
+                if t in slots_on_scalar:
+                    nc.scalar.activation(out=h[:, t, :], in_=bank[:, :width], func=ACT.Square, scale=root_w[:, i : i + 1])
+                else:
+                    scaled = flow.tile([P, width], F32, name=label("scaled", (c, j)), tag="scaled", bufs=1)
+                    nc.vector.tensor_scalar(
+                        out=scaled[:], in0=bank[:, :width], scalar1=root_w[:, i : i + 1], scalar2=None, op0=ALU.mult
+                    )
+                    to_square[h_of(c, j)] = (h[:, t, :], scaled)
             by_slot[(h_of(c, j), half)] = h
 
         def passes(y, slots, groups, new_bank=sum_bank):
@@ -284,14 +288,13 @@ def tile_bucketed_pv_limit_use_h3_kernel(
                 )
 
 
-        pack(disc(0), 0)
-        turn(cash(0), 0, sum_bank(), False)
         turn_weights()
         nc.scalar.activation(out=guess[:], in_=w, func=ACT.Sqrt)
-        turn(cash(0), 1, sum_bank(), False)
-        quantise(cash(0), 0)
-        pack(disc(0), 1)
+        pack(disc(0), 0)
+        turn_both(cash(0), sum_bank)
         nc.vector.reciprocal(out=inverse[:], in_=guess[:])
+        pack(disc(0), 1)
+        quantise(cash(0), 0)
         quantise(disc(0))
         nc.vector.scalar_tensor_tensor(out=half_quotient[:], in0=w, scalar=0.5, in1=inverse[:], op0=ALU.mult, op1=ALU.mult)
         quantise(cash(0), 1)
@@ -309,8 +312,8 @@ def tile_bucketed_pv_limit_use_h3_kernel(
         quantise(cash(2))
         squares(1, 0)
         pack(h_of(0, 0))
-        quantise(h_of(0, 0))
         quantise(bmap(0, 0))
+        quantise(h_of(0, 0))
         turn_both(cash(3), sum_bank, (0,))
         pack(h_of(1, 0))
         quantise(cash(3))
@@ -318,16 +321,16 @@ def tile_bucketed_pv_limit_use_h3_kernel(
 
         y00, y10, y01, y11 = y_of(0, 0), y_of(1, 0), y_of(0, 1), y_of(1, 1)
         to_turn = [bmap(0, c) for c in range(1, POS_GROUPS)] + [bmap(1, c) for c in ALL_GROUPS]
-        to_sort = [bmap(1, c) for c in ALL_GROUPS]
         for step, (c, j) in enumerate([(2, 0), (3, 0), (0, 1)]):
             early, late = to_turn[2 * step], to_turn[2 * step + 1]
+            to_sort = to_turn[2 * step + 2 : 2 * step + 4] if step > 0 else []
             squares(c, j)
             passes(y00, LOW, (step,))
-            turn_both(early, work_bank)
+            turn_both(early, work_bank, (0,) if len(to_sort) == 1 else ())
             passes(y00, HIGH, (step,))
             pack(h_of(c, j))
-            if step > 0:
-                sort_words(to_sort[2 * step - 1])
+            for key in to_sort[:1]:
+                sort_words(key)
             quantise(early)
             turn_both(late, work_bank)
             if step == 0:
@@ -335,8 +338,8 @@ def tile_bucketed_pv_limit_use_h3_kernel(
             quantise(h_of(c, j))
             if step == 0:
                 quantise(disc(1))
-            if step < 2:
-                sort_words(to_sort[2 * step])
+            for key in to_sort[1:]:
+                sort_words(key)
             quantise(late)
 
         squares(1, 1)
@@ -353,21 +356,25 @@ def tile_bucketed_pv_limit_use_h3_kernel(
         before = (y00, HIGH)
         finished = waiting = None
         for c, j, y, slots in [(2, 1, y10, LOW), (3, 1, y10, HIGH), (0, 2, y01, LOW), (1, 2, y01, HIGH), (2, 2, y11, LOW)]:
-            squares(c, j)
+            squares(c, j, None, ALL_SLOTS[:-1] if (c, j) == SHARED_H else ALL_SLOTS)
+            if finished:
+                pack(finished)
             if (y, slots) == (y01, LOW):
                 passes(y, slots, ALL_GROUPS)
             else:
                 slot_sums(y, slots)
             roots(*before)
-            if waiting:
-                store_codes(waiting)
+            if h_of(c, j) in to_square:
+                row, scaled = to_square[h_of(c, j)]
+                nc.vector.tensor_tensor(out=row, in0=scaled[:], in1=scaled[:], op=ALU.mult)
             pack(h_of(c, j))
-            quantise(h_of(c, j))
             if finished:
-                pack(finished)
                 quantise_y(finished)
-            waiting = finished
-            finished = before[0] if before[1] == HIGH else None
+                store_codes(finished)
+            if c % 2:
+                quantise(h_of(c - 1, j))
+                quantise(h_of(c, j))
+            finished, waiting = waiting, before[0] if before[1] == HIGH else None
             before = (y, slots)
         store_scales(span(0), [nc.sync])
 
@@ -377,11 +384,12 @@ def tile_bucketed_pv_limit_use_h3_kernel(
         slot_sums(y11, (3,))
         roots(y11, LOW)
         pack(h_of(3, 2), 0)
-        pack(y01)
+        quantise(h_of(2, 2))
         quantise(h_of(3, 2), 0)
         pack(h_of(3, 2), 1)
-        quantise_y(y01)
+        pack(y01)
         quantise(h_of(3, 2), 1)
+        quantise_y(y01)
 
         pieces = [
             y_of(0, LAST_CHUNK, 0, HALF),

from contextlib import ExitStack

import concourse.mybir as mybir
from concourse.masks import make_identity

POSITIONS, DATES, SCENARIOS, BUCKETS = 2048, 512, 1536, 1024
FLOPS = 2 * POSITIONS * DATES * SCENARIOS + 2 * BUCKETS * POSITIONS * SCENARIOS

F32 = mybir.dt.float32
BF16 = mybir.dt.bfloat16
U32 = mybir.dt.uint32
I32 = mybir.dt.int32
U8 = mybir.dt.uint8
FP8X4 = mybir.dt.float8_e4m3fn_x4
ACT = mybir.ActivationFunctionType
ALU = mybir.AluOpType

P = 128
SLOTS = 4
W = 512
HALF = W // 2
QUARTER = W // 4
POS_GROUPS = POSITIONS // W
BUCKET_GROUPS = BUCKETS // W
LAST_CHUNK = SCENARIOS // W - 1
RUN = 4
ALL_SLOTS = range(SLOTS)
LOW, HIGH = (0, 1), (2, 3)
ALL_GROUPS = range(POS_GROUPS)
SHARED_H = (0, LAST_CHUNK)
ALIVE = {"cash": POS_GROUPS, "disc": LAST_CHUNK + 1, "map": BUCKET_GROUPS * POS_GROUPS, "h": 2 * POS_GROUPS}


def cash(c):
    return ("cash", c)


def disc(j):
    return ("disc", j)


def bmap(g, c):
    return ("map", g, c)


def h_of(c, j):
    return ("h", c, j)


def y_of(g, j, first=0, width=W):
    return ("y", g, j, first, width)


def label(prefix, key):
    return "_".join([prefix] + [str(part) for part in key])


def span(i, width=W):
    return slice(width * i, width * (i + 1))


def tile_bucketed_pv_limit_use_h3_kernel(
    tc, cashflows, discounts, position_weights, bucket_map, limit_weights, out_0, out_1, out_2
):
    nc = tc.nc
    with ExitStack() as ctx:
        keep = ctx.enter_context(tc.tile_pool(name="keep", bufs=1))
        flow = ctx.enter_context(tc.tile_pool(name="flow", bufs=3))
        work_pool = ctx.enter_context(tc.psum_pool(name="work", bufs=4))
        sum_pool = ctx.enter_context(tc.psum_pool(name="sums", bufs=4))
        ctx.enter_context(tc.manual_schedule())

        def work_bank():
            return work_pool.tile([P, W], F32, name="work_bank")

        def sum_bank():
            return sum_pool.tile([P, W], F32, name="sum_bank")

        rows_of = {}
        sorted_words = {}
        by_slot = {}
        packed = {}
        quantised = {}
        y_codes = {}
        to_square = {}
        sums = {}

        def load_rows(key, rows):
            rows_of[key] = keep.tile([P, SLOTS * W], BF16, name=label("rows", key), align_bytes=64)
            nc.sync.dma_start(
                out=rows_of[key][:].rearrange("p (t n) -> p t n", t=SLOTS), in_=rows.rearrange("(p t) n -> p t n", t=SLOTS)
            )

        def load_cash_half(c, half):
            if half == 0:
                rows_of[cash(c)] = keep.tile([P, SLOTS * W], BF16, name=label("rows", cash(c)), align_bytes=64)
            rows = cashflows[span(c), :].rearrange("(p t) n -> p (t n)", t=SLOTS)
            nc.sync.dma_start(out=rows_of[cash(c)][:, span(half, 2 * W)], in_=rows[:, span(half, 2 * W)])

        def load_disc(j, half=None):
            cols = span(j) if half is None else span(2 * j + half, HALF)
            width = cols.stop - cols.start
            tile = keep.tile([P, SLOTS, width], BF16, name=label("rows", ("disc", cols.start)), align_bytes=64)
            nc.sync.dma_start(out=tile[:], in_=discounts[:, cols].rearrange("(p t) n -> p t n", t=SLOTS))
            by_slot[(disc(j), half)] = tile

        def load_map(g, c):
            load_rows(bmap(g, c), bucket_map[span(g), span(c)])

        weight_rows = keep.tile([P, W], BF16, name="weight_rows", align_bytes=64)
        nc.gpsimd.memset(weight_rows[:].bitcast(I32), 0)
        n_rows = POS_GROUPS + BUCKET_GROUPS

        load_cash_half(0, 0)
        nc.sync.dma_start(out=weight_rows[:POS_GROUPS, :], in_=position_weights.rearrange("(c n) -> c n", n=W))
        nc.sync.dma_start(out=weight_rows[POS_GROUPS:n_rows, :], in_=limit_weights.rearrange("(g n) -> g n", n=W))
        load_disc(0, 0)
        load_cash_half(0, 1)
        load_disc(0, 1)
        load_cash_half(1, 0)
        load_cash_half(1, 1)
        load_rows(cash(2), cashflows[span(2), :])
        load_map(0, 0)
        load_rows(cash(3), cashflows[span(3), :])
        load_map(0, 1)
        load_map(0, 2)
        load_disc(1)
        load_map(0, 3)
        for c in ALL_GROUPS:
            load_map(1, c)
        load_disc(2)

        identity = keep.tile([P, P], F32, name="identity")
        make_identity(nc, identity[:])

        n_w = POS_GROUPS * SLOTS
        weights = keep.tile([P, n_rows * SLOTS], BF16, name="weights", align_bytes=64)
        w, limit = weights[:, :n_w], weights[:, n_w:]
        guess = keep.tile([P, n_w], F32, name="guess")
        inverse = keep.tile([P, n_w], F32, name="inverse")
        half_quotient = keep.tile([P, n_w], F32, name="half_quotient")
        root_w = keep.tile([P, n_w], F32, name="root_w")
        limit_squared = keep.tile([P, BUCKET_GROUPS * SLOTS], F32, name="limit_squared")

        def turn_weights():
            bank = work_bank()[:].rearrange("p (u r) -> p u r", r=P)
            words = weight_rows[:].bitcast(F32)
            for u in range(2):
                nc.tensor.transpose(bank[:, u, :], words[:, u::2], identity[:])
            nc.vector.tensor_copy(
                out=weights[:].bitcast(F32).rearrange("p (r u) -> p r u", u=2),
                in_=bank[:, :2, :n_rows].rearrange("p u r -> p r u"),
            )

        y_scales = keep.tile([P, SCENARIOS], U8, name="y_scales", align_bytes=64)

        def sort_words(key):
            tile = flow.tile([P, SLOTS, 2, P], F32, name=label("sorted", key), tag="sorted", align_bytes=64)
            nc.vector.tensor_copy(out=tile[:], in_=rows_of[key][:].bitcast(F32).rearrange("p (t m u) -> p t u m", t=SLOTS, u=2))
            sorted_words[key] = tile

        def turn(key, half, bank, on_vector):
            bank = bank[:].rearrange("p (t u m) -> p t u m", t=2, u=2)
            words = rows_of[key][:].bitcast(F32).rearrange("p (t m u) -> p t u m", t=SLOTS, u=2)
            if key in sorted_words:
                words = sorted_words[key][:]
            for t in range(2):
                for u in range(2):
                    nc.tensor.transpose(bank[:, t, u, :], words[:, 2 * half + t, u, :], identity[:])
            if half == 0:
                packed[key] = flow.tile([P, SLOTS * W], BF16, name=label("turned", key), tag="turned", align_bytes=64)
            out = packed[key][:, span(half, 2 * W)].bitcast(F32).rearrange("p (t m u) -> p t m u", t=2, u=2)
            if on_vector:
                nc.vector.tensor_copy(out=out, in_=bank.rearrange("p t u m -> p t m u"))
            else:
                nc.scalar.copy(out=out, in_=bank.rearrange("p t u m -> p t m u"))

        def turn_both(key, new_bank, halves_on_vector=()):
            for half in range(2):
                turn(key, half, new_bank(), half in halves_on_vector)

        def pack(key, half=None):
            source = by_slot[(key, half)]
            width = source.shape[2]
            if half != 1:
                whole = width if half is None else 2 * width
                packed[key] = flow.tile([P, whole * SLOTS], BF16, name=label("packed", key), tag="packed", align_bytes=64)
            out = packed[key][:, span(half or 0, width * SLOTS)]
            nc.vector.tensor_copy(
                out=out.rearrange("p (c i t) -> p c t i", i=RUN, t=SLOTS),
                in_=source[:].rearrange("p t (c i) -> p c t i", i=RUN),
            )

        def quantise(key, half=None):
            if half != 1:
                kind = key[0]
                codes = flow.tile([P, W], U32, name=label("codes", key), tag="codes_" + kind, bufs=ALIVE[kind], align_bytes=64)
                scales = flow.tile([P, W], U8, name=label("scales", key), tag="scales_" + kind, bufs=ALIVE[kind], align_bytes=64)
                quantised[key] = (codes, scales)
            codes, scales = quantised[key]
            cols, width = (span(0), W) if half is None else (span(half, HALF), HALF)
            nc.vector.quantize_mx(
                out=codes[:, cols].bitcast(FP8X4), scales=scales[:, cols], in_=packed[key][:, span(half or 0, width * SLOTS)]
            )

        def matmul(out, stationary, slot, moving, cols, start, stop):
            lhs, lhs_scales = quantised[stationary]
            rhs, rhs_scales = quantised[moving]
            nc.tensor.matmul_mx(
                out=out,
                lhsT=lhs[:, span(slot, P)].bitcast(FP8X4),
                lhsT_scale=lhs_scales[:, span(slot, P)],
                rhs=rhs[:, cols].bitcast(FP8X4),
                rhs_scale=rhs_scales[:, cols],
                start=start,
                stop=stop,
            )

        def squares(c, j, half=None, slots_on_scalar=ALL_SLOTS):
            cols, width = (span(0), W) if half is None else (span(half, HALF), HALF)
            h = flow.tile([P, SLOTS, width], BF16, name=label("h", (c, j, width)), tag="h", align_bytes=64)
            for t in ALL_SLOTS:
                bank = work_bank()
                matmul(bank[:, :width], cash(c), t, disc(j), cols, True, True)
                i = SLOTS * c + t
                if t in slots_on_scalar:
                    nc.scalar.activation(out=h[:, t, :], in_=bank[:, :width], func=ACT.Square, scale=root_w[:, i : i + 1])
                else:
                    scaled = flow.tile([P, width], F32, name=label("scaled", (c, j)), tag="scaled", bufs=1)
                    nc.vector.tensor_scalar(
                        out=scaled[:], in0=bank[:, :width], scalar1=root_w[:, i : i + 1], scalar2=None, op0=ALU.mult
                    )
                    to_square[h_of(c, j)] = (h[:, t, :], scaled)
            by_slot[(h_of(c, j), half)] = h

        def passes(y, slots, groups, new_bank=sum_bank):
            kind, g, j, first, width = y
            for c in groups:
                for t in slots:
                    if c == 0:
                        sums[(y, t)] = new_bank()
                    cols = slice(first, first + width)
                    matmul(sums[(y, t)][:, :width], bmap(g, c), t, h_of(c, j), cols, c == 0, c == POS_GROUPS - 1)

        def slot_sums(y, slots, new_bank=sum_bank):
            for t in slots:
                passes(y, (t,), ALL_GROUPS, new_bank)

        def roots(y, slots):
            kind, g, j, first, width = y
            if 0 in slots:
                tag, bufs = ("y", 2) if width == W else ("y_piece", 5)
                by_slot[(y, None)] = flow.tile([P, SLOTS, width], F32, name=label("values", y), tag=tag, bufs=bufs)
            values = by_slot[(y, None)]
            rows = out_0[span(g), W * j + first : W * j + first + width].rearrange("(p t) n -> p t n", t=SLOTS)
            together = W // width
            for t in slots:
                i = SLOTS * g + t
                nc.scalar.activation(
                    out=values[:, t, :], in_=sums[(y, t)][:, :width], func=ACT.Sqrt, scale=limit_squared[:, i : i + 1]
                )
                if (t + 1) % together == 0:
                    done = slice(t + 1 - together, t + 1)
                    nc.sync.dma_start(out=rows[:, done, :], in_=values[:, done, :])

        def sums_and_roots(y, new_bank):
            for t in ALL_SLOTS:
                slot_sums(y, (t,), new_bank)
                roots(y, (t,))

        def quantise_y(y):
            kind, g, j, first, width = y
            cols = slice(W * j + first, W * j + first + width)
            codes = flow.tile([P, width], U32, name=label("codes", y), tag="codes_y", bufs=4, align_bytes=64)
            nc.vector.quantize_mx(out=codes[:].bitcast(FP8X4), scales=y_scales[4 * g :, cols], in_=packed[y][:])
            y_codes[y] = codes

        def store_codes(y):
            kind, g, j, first, width = y
            cols = slice(W * j + first, W * j + first + width)
            nc.sync.dma_start(out=out_1[g, :, cols, :].rearrange("p n t -> p (n t)").bitcast(I32), in_=y_codes[y][:].bitcast(I32))

        def store_scales(cols, queues):
            for q in range(4):
                queues[q % len(queues)].dma_start(
                    out=out_2[:, 4 * q : 4 * q + 4, cols].bitcast(I32),
                    in_=y_scales[32 * q : 32 * q + 8, cols].bitcast(I32),
                )


        turn_weights()
        nc.scalar.activation(out=guess[:], in_=w, func=ACT.Sqrt)
        pack(disc(0), 0)
        turn_both(cash(0), sum_bank)
        nc.vector.reciprocal(out=inverse[:], in_=guess[:])
        pack(disc(0), 1)
        quantise(cash(0), 0)
        quantise(disc(0))
        nc.vector.scalar_tensor_tensor(out=half_quotient[:], in0=w, scalar=0.5, in1=inverse[:], op0=ALU.mult, op1=ALU.mult)
        quantise(cash(0), 1)
        nc.vector.scalar_tensor_tensor(out=root_w[:], in0=guess[:], scalar=0.5, in1=half_quotient[:], op0=ALU.mult, op1=ALU.add)
        nc.vector.tensor_tensor(out=limit_squared[:], in0=limit, in1=limit, op=ALU.mult)
        turn_both(cash(1), sum_bank)

        sort_words(cash(2))
        squares(0, 0)
        quantise(cash(1))
        sort_words(bmap(0, 0))
        sort_words(cash(3))
        turn_both(cash(2), sum_bank, (0,))
        turn_both(bmap(0, 0), sum_bank, (0,))
        quantise(cash(2))
        squares(1, 0)
        pack(h_of(0, 0))
        quantise(bmap(0, 0))
        quantise(h_of(0, 0))
        turn_both(cash(3), sum_bank, (0,))
        pack(h_of(1, 0))
        quantise(cash(3))
        quantise(h_of(1, 0))

        y00, y10, y01, y11 = y_of(0, 0), y_of(1, 0), y_of(0, 1), y_of(1, 1)
        to_turn = [bmap(0, c) for c in range(1, POS_GROUPS)] + [bmap(1, c) for c in ALL_GROUPS]
        for step, (c, j) in enumerate([(2, 0), (3, 0), (0, 1)]):
            early, late = to_turn[2 * step], to_turn[2 * step + 1]
            to_sort = to_turn[2 * step + 2 : 2 * step + 4] if step > 0 else []
            squares(c, j)
            passes(y00, LOW, (step,))
            turn_both(early, work_bank, (0,) if len(to_sort) == 1 else ())
            passes(y00, HIGH, (step,))
            pack(h_of(c, j))
            for key in to_sort[:1]:
                sort_words(key)
            quantise(early)
            turn_both(late, work_bank)
            if step == 0:
                pack(disc(1))
            quantise(h_of(c, j))
            if step == 0:
                quantise(disc(1))
            for key in to_sort[1:]:
                sort_words(key)
            quantise(late)

        squares(1, 1)
        passes(y00, LOW, (3,))
        turn_both(to_turn[-1], work_bank, (0, 1))
        passes(y00, HIGH, (3,))
        quantise(to_turn[-1])
        roots(y00, LOW)
        pack(disc(2))
        pack(h_of(1, 1))
        quantise(disc(2))
        quantise(h_of(1, 1))

        before = (y00, HIGH)
        finished = waiting = None
        for c, j, y, slots in [(2, 1, y10, LOW), (3, 1, y10, HIGH), (0, 2, y01, LOW), (1, 2, y01, HIGH), (2, 2, y11, LOW)]:
            squares(c, j, None, ALL_SLOTS[:-1] if (c, j) == SHARED_H else ALL_SLOTS)
            if finished:
                pack(finished)
            if (y, slots) == (y01, LOW):
                passes(y, slots, ALL_GROUPS)
            else:
                slot_sums(y, slots)
            roots(*before)
            if h_of(c, j) in to_square:
                row, scaled = to_square[h_of(c, j)]
                nc.vector.tensor_tensor(out=row, in0=scaled[:], in1=scaled[:], op=ALU.mult)
            pack(h_of(c, j))
            if finished:
                quantise_y(finished)
                store_codes(finished)
            if c % 2:
                quantise(h_of(c - 1, j))
                quantise(h_of(c, j))
            finished, waiting = waiting, before[0] if before[1] == HIGH else None
            before = (y, slots)
        store_scales(span(0), [nc.sync])

        squares(3, 2, 0)
        slot_sums(y11, (2,))
        squares(3, 2, 1)
        slot_sums(y11, (3,))
        roots(y11, LOW)
        pack(h_of(3, 2), 0)
        quantise(h_of(2, 2))
        quantise(h_of(3, 2), 0)
        pack(h_of(3, 2), 1)
        pack(y01)
        quantise(h_of(3, 2), 1)
        quantise_y(y01)

        pieces = [
            y_of(0, LAST_CHUNK, 0, HALF),
            y_of(1, LAST_CHUNK, 0, HALF),
            y_of(0, LAST_CHUNK, HALF, HALF),
            y_of(1, LAST_CHUNK, HALF, QUARTER),
            y_of(1, LAST_CHUNK, HALF + QUARTER, QUARTER),
        ]
        passes(pieces[0], ALL_SLOTS, ALL_GROUPS, work_bank)
        roots(y11, HIGH)
        store_codes(y01)
        roots(pieces[0], ALL_SLOTS)
        pack(y11)
        pack(pieces[0])
        quantise_y(y11)
        quantise_y(pieces[0])
        for k in range(1, len(pieces)):
            new_bank = sum_bank if k % 2 else work_bank
            sums_and_roots(pieces[k], new_bank)
            if k == 1:
                store_codes(y11)
            store_codes(pieces[k - 1])
            pack(pieces[k])
            quantise_y(pieces[k])
        store_codes(pieces[-1])
        store_scales(slice(W, SCENARIOS), [nc.scalar, nc.sync])
